import numpy as np
import ml_dtypes


def mxq(x, axis, fmt="e4m3"):
    dtype, down = {"e4m3": (ml_dtypes.float8_e4m3fn, 7), "e5m2": (ml_dtypes.float8_e5m2, 14)}[fmt]
    v = np.moveaxis(np.asarray(x, np.float32).astype(ml_dtypes.bfloat16).astype(np.float64), axis, -1)
    blocks = v.reshape(v.shape[:-1] + (-1, 32))
    amax = np.abs(blocks).max(-1, keepdims=True)
    byte = np.maximum(np.where(amax > 0, np.frexp(amax)[1] - 1 + 127, 0) - down, 1)
    scale = np.exp2(byte - 127.0)
    codes = (blocks / scale).astype(np.float32).astype(dtype).astype(np.float64)
    return np.moveaxis((codes * scale).reshape(v.shape), -1, axis)


WIDE = False


def mx_kscale(k):
    if not WIDE:
        return np.ones(k)
    levels = np.array([10, -10, 5, -5, 0])
    if k % 512:
        return np.exp2(np.random.permutation(np.resize(levels, k // 32))).repeat(32)
    a = np.empty((k // 512, 16))
    for p in range(k // 512):
        a[p, :8] = np.random.permutation(np.resize(levels, 8))
        for g in range(8):
            far = levels[np.abs(levels - a[p, g]) >= 10]
            a[p, g + 8] = far[np.random.randint(len(far))]
    return np.exp2(a.ravel()).repeat(32)


def f64(x):
    return np.asarray(x).astype(np.float64)


def striped(idx):
    return np.tile(np.asarray(idx).reshape(-1, 16).T, (8, 1)).astype(np.uint16)


def unstriped(offs):
    return offs[:16].T.reshape(-1).astype(np.int64)


E2M1 = np.array([0.0, 0.5, 1.0, 1.5, 2.0, 3.0, 4.0, 6.0, -0.0, -0.5, -1.0, -1.5, -2.0, -3.0, -4.0, -6.0])


def pack_weight(w, fmt):
    k, n = w.shape
    w = f64(np.asarray(w, np.float32).astype(ml_dtypes.bfloat16)).reshape(k // 32, 32, n)
    amax = np.abs(w).max(1)
    if fmt == "e4m3":
        byte = np.frexp(amax)[1] - 1 + 127 - 7
    else:
        mant, ex = np.frexp(amax / 6.0)
        byte = np.where(mant > 0.5, ex, ex - 1) + 127
    byte = np.clip(np.where(amax > 0, byte, 1), 1, 254)
    scaled = (w * np.exp2(127.0 - byte)[:, None, :]).reshape(k, n).astype(np.float32)
    by_word = np.ascontiguousarray(scaled.reshape(k // 512, 128, 4, n).transpose(0, 1, 3, 2))
    if fmt == "e4m3":
        words = by_word.astype(ml_dtypes.float8_e4m3fn).view(np.uint8)
    else:
        c = by_word.astype(ml_dtypes.float4_e2m1fn).view(np.uint8) & 0xF
        words = (c[..., 0::2] | (c[..., 1::2] << 4)).reshape(k // 512, 128, 2 * n)
    return np.ascontiguousarray(words), np.ascontiguousarray(byte.astype(np.uint8).reshape(k // 512, 16, n))


def unpack_weight(words, scales, fmt):
    g, _, n = scales.shape
    words = np.ascontiguousarray(words).reshape(g, 128, n, -1)
    if fmt == "e4m3":
        vals = words.view(ml_dtypes.float8_e4m3fn).astype(np.float64)
    else:
        nib = np.empty((g, 128, n, 4), np.uint8)
        nib[..., 0::2] = words & 0xF
        nib[..., 1::2] = words >> 4
        vals = E2M1[nib]
    vals = vals * np.repeat(np.exp2(scales.astype(np.float64) - 127.0), 8, axis=1)[..., None]
    return vals.transpose(0, 1, 3, 2).reshape(g * 512, n)


def bf(x):
    return np.asarray(x, np.float32).astype(ml_dtypes.bfloat16)


def planes(Y):
    r, m = Y.shape
    b = f64(bf(Y)).reshape(r // 32, 32, m)
    amax = np.abs(b).max(1)
    byte = np.clip(np.where(amax > 0, np.frexp(amax)[1] - 1 + 127 - 7, 1), 1, 254)
    codes = (b * np.exp2(127.0 - byte)[:, None, :]).reshape(r, m).astype(np.float32).astype(ml_dtypes.float8_e4m3fn).view(np.uint8)
    words = codes.reshape(r // 512, 128, 4, m).transpose(0, 1, 3, 2)
    return np.ascontiguousarray(words), np.ascontiguousarray(byte.astype(np.uint8).reshape(r // 512, 16, m))


B, N, T, D, NQ = 1, 512, 2048, 1024, 512


def setup_inputs():
    n = np.random.standard_normal
    idx = np.random.permutation(T)[:B * N]
    s = mx_kscale(D)[:, None]
    kp = pack_weight(n((D, T)) / s, "e2m1")
    return {
        "qT": (n((B, D, NQ)) * s * (1.00 / np.sqrt(D))).astype(np.float32),
        "k_words": np.ascontiguousarray(kp[0].reshape(1, 2, 128, T, 2).transpose(0, 2, 3, 1, 4)).reshape(1, 128, T, 4),
        "k_scales": kp[1],
        "vs": np.tile(np.random.uniform(0.5, 2.0, 2048), (128, 1)).astype(np.float32),
        "ls": (np.random.uniform(7.8, 8.4, (B, 1, NQ))).astype(np.float32),
        "offs": striped(idx),
    }


def reference(qT, k_words, k_scales, vs, ls, offs):
    idx = unstriped(offs)
    pick = lambda x, which: x[:, which].reshape(x.shape[0], B, -1).transpose(1, 0, 2)
    k = unpack_weight(k_words.reshape(1, 128, T, 2, 2).transpose(0, 3, 1, 2, 4).reshape(2, 128, 2 * T), k_scales, "e2m1")
    kg = pick(k, idx)
    qq = mxq(f64(qT), 1, "e4m3")
    a = kg.transpose(0, 2, 1) @ qq
    y = np.exp(a - f64(ls)) * pick(f64(vs), idx)[:, :1, :].transpose(0, 2, 1)
    Y = y[0]
    words, scales = planes(Y)
    return Y, words, scales

@@ -1,0 +1,172 @@
+from contextlib import ExitStack
+
+import concourse.mybir as mybir
+from concourse.masks import make_identity
+
+F32 = mybir.dt.float32
+BF16 = mybir.dt.bfloat16
+I32 = mybir.dt.int32
+U32 = mybir.dt.uint32
+U16 = mybir.dt.uint16
+U8 = mybir.dt.uint8
+FP8X4 = mybir.dt.float8_e4m3fn_x4
+FP4X4 = mybir.dt.float4_e2m1fn_x4
+ACT = mybir.ActivationFunctionType
+ALU = mybir.AluOpType
+
+P = 128
+PACK = 4
+K_PASS = P * PACK
+PASSES = 2
+SLOTS = 512
+TOKENS = 2048
+QUERIES = 512
+CHUNK = 128
+CHUNKS = QUERIES // CHUNK
+HALF = 256
+QUADS = 4
+LIVE_SPAN = 100
+
+FLOPS = 2 * SLOTS * PASSES * K_PASS * QUERIES
+BYTES = (4 * PASSES * K_PASS * QUERIES + P * TOKENS * 4 + PASSES * 16 * TOKENS + 4 * TOKENS + 4 * QUERIES + 2 * P * SLOTS // 16
+         + 4 * SLOTS * QUERIES + SLOTS * QUERIES + 16 * QUERIES)
+
+CAST_ON_SCALAR = ((1, 0), (1, 1))
+SCALE_ON_VECTOR = (2,)
+
+
+def interleave(engine_copy, dst, src):
+    engine_copy(dst.rearrange("p (c i) t -> p c t i", i=4), src.rearrange("p t (c i) -> p c t i", i=4))
+
+
+def tile_attend_plw_vsc_topk_kernel(tc, qT, k_words, k_scales, vs, ls, offs, out_0, out_1, out_2):
+    nc = tc.nc
+
+    def scalar_copy(dst, src):
+        nc.scalar.activation(dst, src, ACT.Copy)
+
+    with ExitStack() as ctx:
+        held = ctx.enter_context(tc.tile_pool(name="held", bufs=1))
+        reuse = ctx.enter_context(tc.tile_pool(name="reuse", bufs=1))
+        ring = ctx.enter_context(tc.tile_pool(name="ring", bufs=4))
+        score_banks = ctx.enter_context(tc.psum_pool(name="score_banks", bufs=4))
+        turn_banks = ctx.enter_context(tc.psum_pool(name="turn_banks", bufs=4))
+
+        offsets = held.tile([P, SLOTS // 16], U16, name="offsets")
+        nc.sync.dma_start(offsets[:], offs)
+
+        WORDS_AT, SCALES_AT, VS_AT = 0, 9216, 14336
+        word_window = reuse.tile([P, TOKENS], I32, name="word_window", offset=WORDS_AT, align_bytes=64)
+        scale_window = reuse.tile([P, TOKENS], U8, name="scale_window", offset=SCALES_AT, align_bytes=64)
+        vs_window = reuse.tile([P, TOKENS], F32, name="vs_window", offset=VS_AT, align_bytes=64)
+
+        nc.sync.dma_start(word_window[:], k_words[0].rearrange("p t b -> p (t b)").bitcast(I32))
+
+        raw = {}
+
+        def load_queries(o, h, tile):
+            rows = qT[0, o * K_PASS:(o + 1) * K_PASS, h * HALF:(h + 1) * HALF]
+            nc.sync.dma_start(tile[:], rows.rearrange("(p j) w -> p j w", j=PACK))
+            raw[o, h] = tile
+
+        load_queries(0, 0, held.tile([P, PACK, HALF], F32, name="raw00"))
+        load_queries(1, 0, held.tile([P, PACK, HALF], F32, name="raw10"))
+
+        nc.vector.memset(scale_window[:].bitcast(I32), 0)
+        for quad in range(QUADS):
+            nc.scalar.dma_start(scale_window[32 * quad:32 * quad + 8, :].bitcast(I32),
+                                k_scales[:, 4 * quad:4 * quad + 4, :].bitcast(I32))
+        plane1 = held.tile([P, SLOTS], U8, name="plane1", align_bytes=64)
+        nc.vector.memset(plane1[:].bitcast(I32), 0)
+        nc.vector.memset(vs_window[:], 0.0)
+        nc.scalar.dma_start(vs_window[0:1, :], vs[0:1, :])
+
+        identity = held.tile([P, P], F32, name="identity")
+        make_identity(nc, identity[:])
+        ls_rows = held.tile([P, P], F32, name="ls_rows")
+        nc.gpsimd.memset(ls_rows[:], 0.0)
+        nc.gpsimd.dma_start(ls_rows[0:CHUNKS, :], ls[0, 0, :].rearrange("(c p) -> c p", p=P))
+
+        plane0 = held.tile([P, SLOTS], U8, name="plane0", align_bytes=64)
+        nc.vector.tensor_copy(plane0[:], scale_window[:].indirect(offsets[:]))
+        nc.sync.dma_start(plane1[0:LIVE_SPAN, :].bitcast(I32), plane0[4:4 + LIVE_SPAN, :].bitcast(I32))
+        key_planes = (plane0, plane1)
+
+        pairs = reuse.tile([P, SLOTS], U32, name="pairs", offset=SCALES_AT - 1024, align_bytes=64)
+        nc.vector.tensor_copy(pairs[:], word_window[:].bitcast(U32).indirect(offsets[:]))
+        key_words = []
+        for o in range(PASSES):
+            words = held.tile([P, 2 * SLOTS], U8, name="key_words%d" % o, align_bytes=64)
+            nc.vector.tensor_copy(words[:].bitcast(U16), pairs[:].bitcast(U16).rearrange("p (n h) -> p n h", h=2)[:, :, o])
+            key_words.append(words)
+
+        load_queries(0, 1, reuse.tile([P, PACK, HALF], F32, name="raw01", offset=SCALES_AT + 1024, align_bytes=64))
+        load_queries(1, 1, reuse.tile([P, PACK, HALF], F32, name="raw11", offset=WORDS_AT, align_bytes=64))
+
+        vs_listed = held.tile([P, SLOTS], F32, name="vs_listed")
+        nc.scalar.activation(vs_listed[:], vs_window[:].indirect(offsets[:]), ACT.Copy)
+
+        ls_turned = turn_banks.tile([P, PACK, P], F32, name="turned")
+        nc.tensor.transpose(ls_turned[:, 0, :], ls_rows[:], identity[:])
+        minus_ls = held.tile([P, CHUNKS], F32, name="minus_ls")
+        nc.scalar.mul(minus_ls[:], ls_turned[:, 0, 0:CHUNKS], -1.0)
+        vs_turned = turn_banks.tile([P, PACK, P], F32, name="turned")
+        for r in range(PACK):
+            nc.tensor.transpose(vs_turned[:, r, :], vs_listed[:, r:SLOTS:PACK], identity[:])
+        vs_columns = held.tile([P, PACK], F32, name="vs_columns")
+        nc.scalar.copy(vs_columns[:], vs_turned[:, :, 0])
+
+        grouped_at = {(0, 0): WORDS_AT + 4096, (0, 1): WORDS_AT + 5120, (1, 0): VS_AT, (1, 1): VS_AT + 1024}
+        y_words = held.tile([P, QUERIES], I32, name="y_words", align_bytes=64)
+        y_plane = held.tile([P, QUERIES], U8, name="y_plane", align_bytes=64)
+        out_rows = out_0.rearrange("(s r) q -> s r q", r=PACK)
+        out_words = out_1[0].rearrange("p q t -> p (q t)").bitcast(I32)
+        scores = {}
+
+        def score(c):
+            bank = score_banks.tile([P, SLOTS], F32, name="scores")
+            for o in range(PASSES):
+                if (o, c) in grouped_at:
+                    grouped = reuse.tile([P, CHUNK, PACK], BF16, name="grouped%d%d" % (o, c), offset=grouped_at[o, c], align_bytes=64)
+                else:
+                    grouped = ring.tile([P, CHUNK, PACK], BF16, name="grouped", align_bytes=64)
+                src = raw[o, c // 2][:, :, (c % 2) * CHUNK:(c % 2 + 1) * CHUNK]
+                interleave(scalar_copy if (o, c) in CAST_ON_SCALAR else nc.vector.tensor_copy, grouped[:], src)
+                codes = held.tile([P, CHUNK], U32, name="q_codes%d%d" % (o, c), align_bytes=64)
+                plane = held.tile([P, CHUNK], U8, name="q_plane%d%d" % (o, c), align_bytes=64)
+                nc.vector.quantize_mx(codes[:].bitcast(FP8X4), plane[:], grouped[:].rearrange("p w t -> p (w t)"))
+                nc.tensor.matmul_mx(out=bank[:], lhsT=codes[:].bitcast(FP8X4), lhsT_scale=plane[:],
+                                    rhs=key_words[o][:].bitcast(FP4X4), rhs_scale=key_planes[o][:],
+                                    start=(o == 0), stop=(o == PASSES - 1))
+            scores[c] = bank
+
+        def weigh(c):
+            cols = slice(c * CHUNK, (c + 1) * CHUNK)
+            e = ring.tile([P, PACK, P], F32, name="e")
+            nc.scalar.activation(e[:], scores[c][:].rearrange("p (s r) -> p r s", r=PACK), ACT.Exp, bias=minus_ls[:, c:c + 1])
+            turned = turn_banks.tile([P, PACK, P], F32, name="turned")
+            for r in range(PACK):
+                nc.tensor.transpose(turned[:, r, :], e[:, r, :], identity[:])
+            y = ring.tile([P, PACK, CHUNK], F32, name="y")
+            if c in SCALE_ON_VECTOR:
+                nc.vector.tensor_tensor(y[:], turned[:], vs_columns[:].unsqueeze(2).to_broadcast([P, PACK, CHUNK]), ALU.mult)
+            else:
+                for r in range(PACK):
+                    nc.scalar.activation(y[:, r, :], turned[:, r, :], ACT.Copy, scale=vs_columns[:, r:r + 1])
+            nc.sync.dma_start(out_rows[:, :, cols], y[:])
+            rounded = ring.tile([P, CHUNK, PACK], BF16, name="rounded", align_bytes=64)
+            interleave(nc.vector.tensor_copy, rounded[:], y[:])
+            nc.vector.quantize_mx(y_words[:, cols].bitcast(FP8X4), y_plane[:, cols], rounded[:].rearrange("p w t -> p (w t)"))
+            if c % 2 == 1:
+                half = slice((c - 1) * CHUNK, (c + 1) * CHUNK)
+                nc.sync.dma_start(out_words[:, half], y_words[:, half])
+
+        score(0)
+        for c in range(1, CHUNKS):
+            score(c)
+            weigh(c - 1)
+        weigh(CHUNKS - 1)
+
+        for quad in range(QUADS):
+            queue = nc.sync if quad % 2 == 0 else nc.scalar
+            queue.dma_start(out_2[0, 4 * quad:4 * quad + 4, :].bitcast(I32), y_plane[32 * quad:32 * quad + 4, :].bitcast(I32))

@@ -1,7 +1,6 @@
 from contextlib import ExitStack
 
 import concourse.mybir as mybir
-from concourse.masks import make_identity
 
 F32 = mybir.dt.float32
 BF16 = mybir.dt.bfloat16
@@ -26,13 +25,13 @@ CHUNKS = QUERIES // CHUNK
 HALF = 256
 QUADS = 4
 LIVE_SPAN = 100
+SHIFT = 16
 
 FLOPS = 2 * SLOTS * PASSES * K_PASS * QUERIES
 BYTES = (4 * PASSES * K_PASS * QUERIES + P * TOKENS * 4 + PASSES * 16 * TOKENS + 4 * TOKENS + 4 * QUERIES + 2 * P * SLOTS // 16
          + 4 * SLOTS * QUERIES + SLOTS * QUERIES + 16 * QUERIES)
 
-CAST_ON_SCALAR = ((1, 0), (1, 1))
-SCALE_ON_VECTOR = (2,)
+SCALE_ON_VECTOR = (1,)
 
 
 def interleave(engine_copy, dst, src):
@@ -49,19 +48,17 @@ def tile_attend_plw_vsc_topk_kernel(tc, qT, k_words, k_scales, vs, ls, offs, out
         held = ctx.enter_context(tc.tile_pool(name="held", bufs=1))
         reuse = ctx.enter_context(tc.tile_pool(name="reuse", bufs=1))
         ring = ctx.enter_context(tc.tile_pool(name="ring", bufs=4))
-        score_banks = ctx.enter_context(tc.psum_pool(name="score_banks", bufs=4))
-        turn_banks = ctx.enter_context(tc.psum_pool(name="turn_banks", bufs=4))
+        score_banks = ctx.enter_context(tc.psum_pool(name="score_banks", bufs=1))
+        shared_bank = ctx.enter_context(tc.psum_pool(name="shared_bank", bufs=1))
+        turn_banks = ctx.enter_context(tc.psum_pool(name="turn_banks", bufs=1))
 
         offsets = held.tile([P, SLOTS // 16], U16, name="offsets")
         nc.sync.dma_start(offsets[:], offs)
 
-        WORDS_AT, SCALES_AT, VS_AT = 0, 9216, 14336
+        WORDS_AT, SCALES_AT, VS_AT, FIRST_AT, LAST_AT = 0, 10240, 17408, 25600, 31744
         word_window = reuse.tile([P, TOKENS], I32, name="word_window", offset=WORDS_AT, align_bytes=64)
         scale_window = reuse.tile([P, TOKENS], U8, name="scale_window", offset=SCALES_AT, align_bytes=64)
         vs_window = reuse.tile([P, TOKENS], F32, name="vs_window", offset=VS_AT, align_bytes=64)
-
-        nc.sync.dma_start(word_window[:], k_words[0].rearrange("p t b -> p (t b)").bitcast(I32))
-
         raw = {}
 
         def load_queries(o, h, tile):
@@ -70,29 +67,64 @@ def tile_attend_plw_vsc_topk_kernel(tc, qT, k_words, k_scales, vs, ls, offs, out
             raw[o, h] = tile
 
         load_queries(0, 0, held.tile([P, PACK, HALF], F32, name="raw00"))
-        load_queries(1, 0, held.tile([P, PACK, HALF], F32, name="raw10"))
-
         nc.vector.memset(scale_window[:].bitcast(I32), 0)
-        for quad in range(QUADS):
-            nc.scalar.dma_start(scale_window[32 * quad:32 * quad + 8, :].bitcast(I32),
-                                k_scales[:, 4 * quad:4 * quad + 4, :].bitcast(I32))
+        by_quad = k_scales.rearrange("o (q r) t -> r q o t", r=4)
+        for r in range(4):
+            nc.sync.dma_start(scale_window[r:P:SHIFT, :].bitcast(I32), by_quad[r].bitcast(I32))
+        nc.vector.memset(vs_window[:], 0.0)
+        nc.sync.dma_start(vs_window[0:1, :], vs[0:1, :])
+        nc.sync.dma_start(word_window[:], k_words[0].rearrange("p t b -> p (t b)").bitcast(I32))
+        ls_rows = held.tile([P, P], F32, name="ls_rows")
+        nc.vector.memset(ls_rows[:], 0.0)
+        nc.sync.dma_start(ls_rows[0:CHUNKS, :], ls[0, 0, :].rearrange("(c p) -> c p", p=P))
         plane1 = held.tile([P, SLOTS], U8, name="plane1", align_bytes=64)
         nc.vector.memset(plane1[:].bitcast(I32), 0)
-        nc.vector.memset(vs_window[:], 0.0)
-        nc.scalar.dma_start(vs_window[0:1, :], vs[0:1, :])
+        load_queries(1, 0, reuse.tile([P, PACK, HALF], F32, name="raw10", offset=FIRST_AT, align_bytes=64))
+        load_queries(0, 1, held.tile([P, PACK, HALF], F32, name="raw01"))
 
+        ones = held.tile([P, P], F32, name="ones")
+        nc.vector.memset(ones[:], 1.0)
+        counts = held.tile([P, P], F32, name="counts", align_bytes=64)
+        nc.vector.tensor_tensor_scan(counts[:], ones[:], ones[:], 0.0, ALU.mult, ALU.add)
+        counts_turned = held.tile([P, P], F32, name="counts_turned", align_bytes=64)
+        nc.vector.transpose(counts_turned[:], counts[:])
         identity = held.tile([P, P], F32, name="identity")
-        make_identity(nc, identity[:])
-        ls_rows = held.tile([P, P], F32, name="ls_rows")
-        nc.gpsimd.memset(ls_rows[:], 0.0)
-        nc.gpsimd.dma_start(ls_rows[0:CHUNKS, :], ls[0, 0, :].rearrange("(c p) -> c p", p=P))
+        for quad in range(QUADS):
+            rows = slice(32 * quad, 32 * quad + 32)
+            nc.vector.tensor_scalar(identity[rows, :], counts[rows, :], counts_turned[rows, 32 * quad:32 * quad + 1], None, ALU.is_equal)
+
+        queries = {}
+
+        def quantise_queries(o, first, count, engine_copy, grouped_at=None, codes_at=None):
+            width = count * CHUNK
+            name = "%d%d" % (o, first)
+            if grouped_at is None:
+                grouped = held.tile([P, width, PACK], BF16, name="grouped" + name, align_bytes=64)
+            else:
+                grouped = reuse.tile([P, width, PACK], BF16, name="grouped" + name, offset=grouped_at, align_bytes=64)
+            start = (first % 2) * CHUNK
+            interleave(engine_copy, grouped[:], raw[o, first // 2][:, :, start:start + width])
+            if codes_at is None:
+                codes = held.tile([P, width], U32, name="q_codes" + name, align_bytes=64)
+            else:
+                codes = reuse.tile([P, width], U32, name="q_codes" + name, offset=codes_at, align_bytes=64)
+            plane = held.tile([P, width], U8, name="q_plane" + name, align_bytes=64)
+            nc.vector.quantize_mx(codes[:].bitcast(FP8X4), plane[:], grouped[:].rearrange("p w t -> p (w t)"))
+            for i in range(count):
+                cols = slice(i * CHUNK, (i + 1) * CHUNK)
+                queries[o, first + i] = (codes[:, cols], plane[:, cols])
 
         plane0 = held.tile([P, SLOTS], U8, name="plane0", align_bytes=64)
         nc.vector.tensor_copy(plane0[:], scale_window[:].indirect(offsets[:]))
-        nc.sync.dma_start(plane1[0:LIVE_SPAN, :].bitcast(I32), plane0[4:4 + LIVE_SPAN, :].bitcast(I32))
+        nc.sync.dma_start(plane1[0:LIVE_SPAN, :].bitcast(I32), plane0[SHIFT:SHIFT + LIVE_SPAN, :].bitcast(I32))
         key_planes = (plane0, plane1)
+        load_queries(1, 1, reuse.tile([P, PACK, HALF], F32, name="raw11", offset=SCALES_AT + 1088, align_bytes=64))
+        quantise_queries(0, 0, 2, scalar_copy, codes_at=SCALES_AT + 64)
 
-        pairs = reuse.tile([P, SLOTS], U32, name="pairs", offset=SCALES_AT - 1024, align_bytes=64)
+        vs_listed = held.tile([P, SLOTS], F32, name="vs_listed")
+        nc.scalar.activation(vs_listed[:], vs_window[:].indirect(offsets[:]), ACT.Copy)
+
+        pairs = reuse.tile([P, SLOTS], U32, name="pairs", offset=SCALES_AT + 64 - 4 * SLOTS, align_bytes=64)
         nc.vector.tensor_copy(pairs[:], word_window[:].bitcast(U32).indirect(offsets[:]))
         key_words = []
         for o in range(PASSES):
@@ -100,72 +132,75 @@ def tile_attend_plw_vsc_topk_kernel(tc, qT, k_words, k_scales, vs, ls, offs, out
             nc.vector.tensor_copy(words[:].bitcast(U16), pairs[:].bitcast(U16).rearrange("p (n h) -> p n h", h=2)[:, :, o])
             key_words.append(words)
 
-        load_queries(0, 1, reuse.tile([P, PACK, HALF], F32, name="raw01", offset=SCALES_AT + 1024, align_bytes=64))
-        load_queries(1, 1, reuse.tile([P, PACK, HALF], F32, name="raw11", offset=WORDS_AT, align_bytes=64))
 
-        vs_listed = held.tile([P, SLOTS], F32, name="vs_listed")
-        nc.scalar.activation(vs_listed[:], vs_window[:].indirect(offsets[:]), ACT.Copy)
-
-        ls_turned = turn_banks.tile([P, PACK, P], F32, name="turned")
+        ls_turned = turn_banks.tile([P, PACK, P], F32, name="ls_turned")
         nc.tensor.transpose(ls_turned[:, 0, :], ls_rows[:], identity[:])
         minus_ls = held.tile([P, CHUNKS], F32, name="minus_ls")
         nc.scalar.mul(minus_ls[:], ls_turned[:, 0, 0:CHUNKS], -1.0)
-        vs_turned = turn_banks.tile([P, PACK, P], F32, name="turned")
+        vs_turned = shared_bank.tile([P, PACK, P], F32, name="shared")
         for r in range(PACK):
             nc.tensor.transpose(vs_turned[:, r, :], vs_listed[:, r:SLOTS:PACK], identity[:])
-        vs_columns = held.tile([P, PACK], F32, name="vs_columns")
-        nc.scalar.copy(vs_columns[:], vs_turned[:, :, 0])
+        vs_columns = reuse.tile([P, PACK], F32, name="vs_columns", offset=FIRST_AT, align_bytes=64)
 
-        grouped_at = {(0, 0): WORDS_AT + 4096, (0, 1): WORDS_AT + 5120, (1, 0): VS_AT, (1, 1): VS_AT + 1024}
         y_words = held.tile([P, QUERIES], I32, name="y_words", align_bytes=64)
         y_plane = held.tile([P, QUERIES], U8, name="y_plane", align_bytes=64)
         out_rows = out_0.rearrange("(s r) q -> s r q", r=PACK)
         out_words = out_1[0].rearrange("p q t -> p (q t)").bitcast(I32)
-        scores = {}
+        weights = {}
 
         def score(c):
-            bank = score_banks.tile([P, SLOTS], F32, name="scores")
+            if c % 2 == 1:
+                bank = shared_bank.tile([P, SLOTS], F32, name="shared")
+            else:
+                bank = score_banks.tile([P, SLOTS], F32, name="scores")
             for o in range(PASSES):
-                if (o, c) in grouped_at:
-                    grouped = reuse.tile([P, CHUNK, PACK], BF16, name="grouped%d%d" % (o, c), offset=grouped_at[o, c], align_bytes=64)
-                else:
-                    grouped = ring.tile([P, CHUNK, PACK], BF16, name="grouped", align_bytes=64)
-                src = raw[o, c // 2][:, :, (c % 2) * CHUNK:(c % 2 + 1) * CHUNK]
-                interleave(scalar_copy if (o, c) in CAST_ON_SCALAR else nc.vector.tensor_copy, grouped[:], src)
-                codes = held.tile([P, CHUNK], U32, name="q_codes%d%d" % (o, c), align_bytes=64)
-                plane = held.tile([P, CHUNK], U8, name="q_plane%d%d" % (o, c), align_bytes=64)
-                nc.vector.quantize_mx(codes[:].bitcast(FP8X4), plane[:], grouped[:].rearrange("p w t -> p (w t)"))
-                nc.tensor.matmul_mx(out=bank[:], lhsT=codes[:].bitcast(FP8X4), lhsT_scale=plane[:],
+                codes, plane = queries[o, c]
+                nc.tensor.matmul_mx(out=bank[:], lhsT=codes.bitcast(FP8X4), lhsT_scale=plane,
                                     rhs=key_words[o][:].bitcast(FP4X4), rhs_scale=key_planes[o][:],
                                     start=(o == 0), stop=(o == PASSES - 1))
-            scores[c] = bank
-
-        def weigh(c):
-            cols = slice(c * CHUNK, (c + 1) * CHUNK)
             e = ring.tile([P, PACK, P], F32, name="e")
-            nc.scalar.activation(e[:], scores[c][:].rearrange("p (s r) -> p r s", r=PACK), ACT.Exp, bias=minus_ls[:, c:c + 1])
-            turned = turn_banks.tile([P, PACK, P], F32, name="turned")
+            nc.scalar.activation(e[:], bank[:].rearrange("p (s r) -> p r s", r=PACK), ACT.Exp, bias=minus_ls[:, c:c + 1])
+            weights[c] = e
+
+        def hand_on(c):
+            cols = slice(c * CHUNK, (c + 1) * CHUNK)
+            turned = turn_banks.tile([P, PACK, P], F32, name="turned%d" % max(c, 1))
             for r in range(PACK):
-                nc.tensor.transpose(turned[:, r, :], e[:, r, :], identity[:])
-            y = ring.tile([P, PACK, CHUNK], F32, name="y")
+                nc.tensor.transpose(turned[:, r, :], weights[c][:, r, :], identity[:])
+            if c == 1:
+                y = reuse.tile([P, PACK, CHUNK], F32, name="y1", offset=LAST_AT + 512, align_bytes=64)
+            else:
+                y = ring.tile([P, PACK, CHUNK], F32, name="y")
             if c in SCALE_ON_VECTOR:
                 nc.vector.tensor_tensor(y[:], turned[:], vs_columns[:].unsqueeze(2).to_broadcast([P, PACK, CHUNK]), ALU.mult)
             else:
                 for r in range(PACK):
                     nc.scalar.activation(y[:, r, :], turned[:, r, :], ACT.Copy, scale=vs_columns[:, r:r + 1])
             nc.sync.dma_start(out_rows[:, :, cols], y[:])
-            rounded = ring.tile([P, CHUNK, PACK], BF16, name="rounded", align_bytes=64)
+            if c == 0:
+                rounded = reuse.tile([P, CHUNK, PACK], BF16, name="rounded0", offset=LAST_AT - 512, align_bytes=64)
+            else:
+                rounded = ring.tile([P, CHUNK, PACK], BF16, name="rounded", align_bytes=64)
             interleave(nc.vector.tensor_copy, rounded[:], y[:])
             nc.vector.quantize_mx(y_words[:, cols].bitcast(FP8X4), y_plane[:, cols], rounded[:].rearrange("p w t -> p (w t)"))
             if c % 2 == 1:
                 half = slice((c - 1) * CHUNK, (c + 1) * CHUNK)
                 nc.sync.dma_start(out_words[:, half], y_words[:, half])
 
+        quantise_queries(1, 0, 1, scalar_copy, grouped_at=VS_AT)
+        quantise_queries(1, 1, 1, scalar_copy, grouped_at=VS_AT + 1024)
+        nc.scalar.copy(vs_columns[:], vs_turned[:, :, 0])
         score(0)
-        for c in range(1, CHUNKS):
-            score(c)
-            weigh(c - 1)
-        weigh(CHUNKS - 1)
+        score(1)
+        quantise_queries(0, 2, 2, nc.vector.tensor_copy, grouped_at=VS_AT - 1024)
+        quantise_queries(1, 2, 1, nc.vector.tensor_copy)
+        quantise_queries(1, 3, 1, nc.vector.tensor_copy, grouped_at=LAST_AT)
+        hand_on(0)
+        score(2)
+        hand_on(1)
+        score(3)
+        hand_on(2)
+        hand_on(3)
 
         for quad in range(QUADS):
             queue = nc.sync if quad % 2 == 0 else nc.scalar

@@ -31,7 +31,7 @@ FLOPS = 2 * SLOTS * PASSES * K_PASS * QUERIES
 BYTES = (4 * PASSES * K_PASS * QUERIES + P * TOKENS * 4 + PASSES * 16 * TOKENS + 4 * TOKENS + 4 * QUERIES + 2 * P * SLOTS // 16
          + 4 * SLOTS * QUERIES + SLOTS * QUERIES + 16 * QUERIES)
 
-SCALE_ON_VECTOR = (1,)
+SHARES = (((0, 4, False),), ((0, 4, True),), ((0, 4, False),), ((0, 2, False), (2, 2, True)))
 
 
 def interleave(engine_copy, dst, src):
@@ -153,29 +153,34 @@ def tile_attend_plw_vsc_topk_kernel(tc, qT, k_words, k_scales, vs, ls, offs, out
                 bank = shared_bank.tile([P, SLOTS], F32, name="shared")
             else:
                 bank = score_banks.tile([P, SLOTS], F32, name="scores")
-            for o in range(PASSES):
+            order = (1, 0) if c == 1 else (0, 1)
+            for o in order:
                 codes, plane = queries[o, c]
                 nc.tensor.matmul_mx(out=bank[:], lhsT=codes.bitcast(FP8X4), lhsT_scale=plane,
                                     rhs=key_words[o][:].bitcast(FP4X4), rhs_scale=key_planes[o][:],
-                                    start=(o == 0), stop=(o == PASSES - 1))
+                                    start=(o == order[0]), stop=(o == order[-1]))
             e = ring.tile([P, PACK, P], F32, name="e")
-            nc.scalar.activation(e[:], bank[:].rearrange("p (s r) -> p r s", r=PACK), ACT.Exp, bias=minus_ls[:, c:c + 1])
+            dealt = bank[:].rearrange("p (s r) -> p r s", r=PACK)
+            for places in ((slice(0, 2), slice(2, 4)) if c == CHUNKS - 1 else (slice(0, 4),)):
+                nc.scalar.activation(e[:, places, :], dealt[:, places, :], ACT.Exp, bias=minus_ls[:, c:c + 1])
             weights[c] = e
 
         def hand_on(c):
             cols = slice(c * CHUNK, (c + 1) * CHUNK)
-            turned = turn_banks.tile([P, PACK, P], F32, name="turned%d" % max(c, 1))
-            for r in range(PACK):
-                nc.tensor.transpose(turned[:, r, :], weights[c][:, r, :], identity[:])
             if c == 1:
                 y = reuse.tile([P, PACK, CHUNK], F32, name="y1", offset=LAST_AT + 512, align_bytes=64)
             else:
                 y = ring.tile([P, PACK, CHUNK], F32, name="y")
-            if c in SCALE_ON_VECTOR:
-                nc.vector.tensor_tensor(y[:], turned[:], vs_columns[:].unsqueeze(2).to_broadcast([P, PACK, CHUNK]), ALU.mult)
-            else:
-                for r in range(PACK):
-                    nc.scalar.activation(y[:, r, :], turned[:, r, :], ACT.Copy, scale=vs_columns[:, r:r + 1])
+            for first, count, on_vector in SHARES[c]:
+                turned = turn_banks.tile([P, PACK, P], F32, name="turned%d%d" % (max(c, 1), first))
+                for i in range(count):
+                    nc.tensor.transpose(turned[:, i, :], weights[c][:, first + i, :], identity[:])
+                if on_vector:
+                    factors = vs_columns[:, first:first + count].unsqueeze(2).to_broadcast([P, count, CHUNK])
+                    nc.vector.tensor_tensor(y[:, first:first + count, :], turned[:, 0:count, :], factors, ALU.mult)
+                else:
+                    for i in range(count):
+                        nc.scalar.activation(y[:, first + i, :], turned[:, i, :], ACT.Copy, scale=vs_columns[:, first + i:first + i + 1])
             nc.sync.dma_start(out_rows[:, :, cols], y[:])
             if c == 0:
                 rounded = reuse.tile([P, CHUNK, PACK], BF16, name="rounded0", offset=LAST_AT - 512, align_bytes=64)

from contextlib import ExitStack

import concourse.mybir as mybir

F32 = mybir.dt.float32
BF16 = mybir.dt.bfloat16
I32 = mybir.dt.int32
U32 = mybir.dt.uint32
U16 = mybir.dt.uint16
U8 = mybir.dt.uint8
FP8X4 = mybir.dt.float8_e4m3fn_x4
FP4X4 = mybir.dt.float4_e2m1fn_x4
ACT = mybir.ActivationFunctionType
ALU = mybir.AluOpType

P = 128
PACK = 4
K_PASS = P * PACK
PASSES = 2
SLOTS = 512
TOKENS = 2048
QUERIES = 512
CHUNK = 128
CHUNKS = QUERIES // CHUNK
HALF = 256
QUADS = 4
LIVE_SPAN = 100
SHIFT = 16

FLOPS = 2 * SLOTS * PASSES * K_PASS * QUERIES
BYTES = (4 * PASSES * K_PASS * QUERIES + P * TOKENS * 4 + PASSES * 16 * TOKENS + 4 * TOKENS + 4 * QUERIES + 2 * P * SLOTS // 16
         + 4 * SLOTS * QUERIES + SLOTS * QUERIES + 16 * QUERIES)

SHARES = (((0, 4, False),), ((0, 4, True),), ((0, 4, False),), ((0, 2, False), (2, 2, True)))


def interleave(engine_copy, dst, src):
    engine_copy(dst.rearrange("p (c i) t -> p c t i", i=4), src.rearrange("p t (c i) -> p c t i", i=4))


def tile_attend_plw_vsc_topk_kernel(tc, qT, k_words, k_scales, vs, ls, offs, out_0, out_1, out_2):
    nc = tc.nc

    def scalar_copy(dst, src):
        nc.scalar.activation(dst, src, ACT.Copy)

    with ExitStack() as ctx:
        held = ctx.enter_context(tc.tile_pool(name="held", bufs=1))
        reuse = ctx.enter_context(tc.tile_pool(name="reuse", bufs=1))
        ring = ctx.enter_context(tc.tile_pool(name="ring", bufs=4))
        score_banks = ctx.enter_context(tc.psum_pool(name="score_banks", bufs=1))
        shared_bank = ctx.enter_context(tc.psum_pool(name="shared_bank", bufs=1))
        turn_banks = ctx.enter_context(tc.psum_pool(name="turn_banks", bufs=1))

        offsets = held.tile([P, SLOTS // 16], U16, name="offsets")
        nc.sync.dma_start(offsets[:], offs)

        WORDS_AT, SCALES_AT, VS_AT, FIRST_AT, LAST_AT = 0, 10240, 17408, 25600, 31744
        word_window = reuse.tile([P, TOKENS], I32, name="word_window", offset=WORDS_AT, align_bytes=64)
        scale_window = reuse.tile([P, TOKENS], U8, name="scale_window", offset=SCALES_AT, align_bytes=64)
        vs_window = reuse.tile([P, TOKENS], F32, name="vs_window", offset=VS_AT, align_bytes=64)
        raw = {}

        def load_queries(o, h, tile):
            rows = qT[0, o * K_PASS:(o + 1) * K_PASS, h * HALF:(h + 1) * HALF]
            nc.sync.dma_start(tile[:], rows.rearrange("(p j) w -> p j w", j=PACK))
            raw[o, h] = tile

        load_queries(0, 0, held.tile([P, PACK, HALF], F32, name="raw00"))
        nc.vector.memset(scale_window[:].bitcast(I32), 0)
        by_quad = k_scales.rearrange("o (q r) t -> r q o t", r=4)
        for r in range(4):
            nc.sync.dma_start(scale_window[r:P:SHIFT, :].bitcast(I32), by_quad[r].bitcast(I32))
        nc.vector.memset(vs_window[:], 0.0)
        nc.sync.dma_start(vs_window[0:1, :], vs[0:1, :])
        nc.sync.dma_start(word_window[:], k_words[0].rearrange("p t b -> p (t b)").bitcast(I32))
        ls_rows = held.tile([P, P], F32, name="ls_rows")
        nc.vector.memset(ls_rows[:], 0.0)
        nc.sync.dma_start(ls_rows[0:CHUNKS, :], ls[0, 0, :].rearrange("(c p) -> c p", p=P))
        plane1 = held.tile([P, SLOTS], U8, name="plane1", align_bytes=64)
        nc.vector.memset(plane1[:].bitcast(I32), 0)
        load_queries(1, 0, reuse.tile([P, PACK, HALF], F32, name="raw10", offset=FIRST_AT, align_bytes=64))
        load_queries(0, 1, held.tile([P, PACK, HALF], F32, name="raw01"))

        ones = held.tile([P, P], F32, name="ones")
        nc.vector.memset(ones[:], 1.0)
        counts = held.tile([P, P], F32, name="counts", align_bytes=64)
        nc.vector.tensor_tensor_scan(counts[:], ones[:], ones[:], 0.0, ALU.mult, ALU.add)
        counts_turned = held.tile([P, P], F32, name="counts_turned", align_bytes=64)
        nc.vector.transpose(counts_turned[:], counts[:])
        identity = held.tile([P, P], F32, name="identity")
        for quad in range(QUADS):
            rows = slice(32 * quad, 32 * quad + 32)
            nc.vector.tensor_scalar(identity[rows, :], counts[rows, :], counts_turned[rows, 32 * quad:32 * quad + 1], None, ALU.is_equal)

        queries = {}

        def quantise_queries(o, first, count, engine_copy, grouped_at=None, codes_at=None):
            width = count * CHUNK
            name = "%d%d" % (o, first)
            if grouped_at is None:
                grouped = held.tile([P, width, PACK], BF16, name="grouped" + name, align_bytes=64)
            else:
                grouped = reuse.tile([P, width, PACK], BF16, name="grouped" + name, offset=grouped_at, align_bytes=64)
            start = (first % 2) * CHUNK
            interleave(engine_copy, grouped[:], raw[o, first // 2][:, :, start:start + width])
            if codes_at is None:
                codes = held.tile([P, width], U32, name="q_codes" + name, align_bytes=64)
            else:
                codes = reuse.tile([P, width], U32, name="q_codes" + name, offset=codes_at, align_bytes=64)
            plane = held.tile([P, width], U8, name="q_plane" + name, align_bytes=64)
            nc.vector.quantize_mx(codes[:].bitcast(FP8X4), plane[:], grouped[:].rearrange("p w t -> p (w t)"))
            for i in range(count):
                cols = slice(i * CHUNK, (i + 1) * CHUNK)
                queries[o, first + i] = (codes[:, cols], plane[:, cols])

        plane0 = held.tile([P, SLOTS], U8, name="plane0", align_bytes=64)
        nc.vector.tensor_copy(plane0[:], scale_window[:].indirect(offsets[:]))
        nc.sync.dma_start(plane1[0:LIVE_SPAN, :].bitcast(I32), plane0[SHIFT:SHIFT + LIVE_SPAN, :].bitcast(I32))
        key_planes = (plane0, plane1)
        load_queries(1, 1, reuse.tile([P, PACK, HALF], F32, name="raw11", offset=SCALES_AT + 1088, align_bytes=64))
        quantise_queries(0, 0, 2, scalar_copy, codes_at=SCALES_AT + 64)

        vs_listed = held.tile([P, SLOTS], F32, name="vs_listed")
        nc.scalar.activation(vs_listed[:], vs_window[:].indirect(offsets[:]), ACT.Copy)

        pairs = reuse.tile([P, SLOTS], U32, name="pairs", offset=SCALES_AT + 64 - 4 * SLOTS, align_bytes=64)
        nc.vector.tensor_copy(pairs[:], word_window[:].bitcast(U32).indirect(offsets[:]))
        key_words = []
        for o in range(PASSES):
            words = held.tile([P, 2 * SLOTS], U8, name="key_words%d" % o, align_bytes=64)
            nc.vector.tensor_copy(words[:].bitcast(U16), pairs[:].bitcast(U16).rearrange("p (n h) -> p n h", h=2)[:, :, o])
            key_words.append(words)


        ls_turned = turn_banks.tile([P, PACK, P], F32, name="ls_turned")
        nc.tensor.transpose(ls_turned[:, 0, :], ls_rows[:], identity[:])
        minus_ls = held.tile([P, CHUNKS], F32, name="minus_ls")
        nc.scalar.mul(minus_ls[:], ls_turned[:, 0, 0:CHUNKS], -1.0)
        vs_turned = shared_bank.tile([P, PACK, P], F32, name="shared")
        for r in range(PACK):
            nc.tensor.transpose(vs_turned[:, r, :], vs_listed[:, r:SLOTS:PACK], identity[:])
        vs_columns = reuse.tile([P, PACK], F32, name="vs_columns", offset=FIRST_AT, align_bytes=64)

        y_words = held.tile([P, QUERIES], I32, name="y_words", align_bytes=64)
        y_plane = held.tile([P, QUERIES], U8, name="y_plane", align_bytes=64)
        out_rows = out_0.rearrange("(s r) q -> s r q", r=PACK)
        out_words = out_1[0].rearrange("p q t -> p (q t)").bitcast(I32)
        weights = {}

        def score(c):
            if c % 2 == 1:
                bank = shared_bank.tile([P, SLOTS], F32, name="shared")
            else:
                bank = score_banks.tile([P, SLOTS], F32, name="scores")
            order = (1, 0) if c == 1 else (0, 1)
            for o in order:
                codes, plane = queries[o, c]
                nc.tensor.matmul_mx(out=bank[:], lhsT=codes.bitcast(FP8X4), lhsT_scale=plane,
                                    rhs=key_words[o][:].bitcast(FP4X4), rhs_scale=key_planes[o][:],
                                    start=(o == order[0]), stop=(o == order[-1]))
            e = ring.tile([P, PACK, P], F32, name="e")
            dealt = bank[:].rearrange("p (s r) -> p r s", r=PACK)
            for places in ((slice(0, 2), slice(2, 4)) if c == CHUNKS - 1 else (slice(0, 4),)):
                nc.scalar.activation(e[:, places, :], dealt[:, places, :], ACT.Exp, bias=minus_ls[:, c:c + 1])
            weights[c] = e

        def hand_on(c):
            cols = slice(c * CHUNK, (c + 1) * CHUNK)
            if c == 1:
                y = reuse.tile([P, PACK, CHUNK], F32, name="y1", offset=LAST_AT + 512, align_bytes=64)
            else:
                y = ring.tile([P, PACK, CHUNK], F32, name="y")
            for first, count, on_vector in SHARES[c]:
                turned = turn_banks.tile([P, PACK, P], F32, name="turned%d%d" % (max(c, 1), first))
                for i in range(count):
                    nc.tensor.transpose(turned[:, i, :], weights[c][:, first + i, :], identity[:])
                if on_vector:
                    factors = vs_columns[:, first:first + count].unsqueeze(2).to_broadcast([P, count, CHUNK])
                    nc.vector.tensor_tensor(y[:, first:first + count, :], turned[:, 0:count, :], factors, ALU.mult)
                else:
                    for i in range(count):
                        nc.scalar.activation(y[:, first + i, :], turned[:, i, :], ACT.Copy, scale=vs_columns[:, first + i:first + i + 1])
            nc.sync.dma_start(out_rows[:, :, cols], y[:])
            if c == 0:
                rounded = reuse.tile([P, CHUNK, PACK], BF16, name="rounded0", offset=LAST_AT - 512, align_bytes=64)
            else:
                rounded = ring.tile([P, CHUNK, PACK], BF16, name="rounded", align_bytes=64)
            interleave(nc.vector.tensor_copy, rounded[:], y[:])
            nc.vector.quantize_mx(y_words[:, cols].bitcast(FP8X4), y_plane[:, cols], rounded[:].rearrange("p w t -> p (w t)"))
            if c % 2 == 1:
                half = slice((c - 1) * CHUNK, (c + 1) * CHUNK)
                nc.sync.dma_start(out_words[:, half], y_words[:, half])

        quantise_queries(1, 0, 1, scalar_copy, grouped_at=VS_AT)
        quantise_queries(1, 1, 1, scalar_copy, grouped_at=VS_AT + 1024)
        nc.scalar.copy(vs_columns[:], vs_turned[:, :, 0])
        score(0)
        score(1)
        quantise_queries(0, 2, 2, nc.vector.tensor_copy, grouped_at=VS_AT - 1024)
        quantise_queries(1, 2, 1, nc.vector.tensor_copy)
        quantise_queries(1, 3, 1, nc.vector.tensor_copy, grouped_at=LAST_AT)
        hand_on(0)
        score(2)
        hand_on(1)
        score(3)
        hand_on(2)
        hand_on(3)

        for quad in range(QUADS):
            queue = nc.sync if quad % 2 == 0 else nc.scalar
            queue.dma_start(out_2[0, 4 * quad:4 * quad + 4, :].bitcast(I32), y_plane[32 * quad:32 * quad + 4, :].bitcast(I32))
